import numpy as np
import ml_dtypes


def mxq(x, axis, fmt="e4m3"):
    dtype, down = {"e4m3": (ml_dtypes.float8_e4m3fn, 7), "e5m2": (ml_dtypes.float8_e5m2, 14)}[fmt]
    v = np.moveaxis(np.asarray(x, np.float32).astype(ml_dtypes.bfloat16).astype(np.float64), axis, -1)
    blocks = v.reshape(v.shape[:-1] + (-1, 32))
    amax = np.abs(blocks).max(-1, keepdims=True)
    byte = np.maximum(np.where(amax > 0, np.frexp(amax)[1] - 1 + 127, 0) - down, 1)
    scale = np.exp2(byte - 127.0)
    codes = (blocks / scale).astype(np.float32).astype(dtype).astype(np.float64)
    return np.moveaxis((codes * scale).reshape(v.shape), -1, axis)


WIDE = False


def mx_kscale(k):
    if not WIDE:
        return np.ones(k)
    levels = np.array([10, -10, 5, -5, 0])
    if k % 512:
        return np.exp2(np.random.permutation(np.resize(levels, k // 32))).repeat(32)
    a = np.empty((k // 512, 16))
    for p in range(k // 512):
        a[p, :8] = np.random.permutation(np.resize(levels, 8))
        for g in range(8):
            far = levels[np.abs(levels - a[p, g]) >= 10]
            a[p, g + 8] = far[np.random.randint(len(far))]
    return np.exp2(a.ravel()).repeat(32)


def f64(x):
    return np.asarray(x).astype(np.float64)


def striped(idx):
    return np.tile(idx.reshape(-1, 16).T, (8, 1)).astype(np.uint16)


def unstriped(offs):
    return offs[:16].T.reshape(-1).astype(np.int64)


E2M1 = np.array([0.0, 0.5, 1.0, 1.5, 2.0, 3.0, 4.0, 6.0, -0.0, -0.5, -1.0, -1.5, -2.0, -3.0, -4.0, -6.0])


def pack_weight(w, fmt):
    k, n = w.shape
    w = f64(np.asarray(w, np.float32).astype(ml_dtypes.bfloat16)).reshape(k // 32, 32, n)
    amax = np.abs(w).max(1)
    if fmt == "e4m3":
        byte = np.frexp(amax)[1] - 1 + 127 - 7
    else:
        mant, ex = np.frexp(amax / 6.0)
        byte = np.where(mant > 0.5, ex, ex - 1) + 127
    byte = np.clip(np.where(amax > 0, byte, 1), 1, 254)
    scaled = (w * np.exp2(127.0 - byte)[:, None, :]).reshape(k, n).astype(np.float32)
    by_word = np.ascontiguousarray(scaled.reshape(k // 512, 128, 4, n).transpose(0, 1, 3, 2))
    if fmt == "e4m3":
        words = by_word.astype(ml_dtypes.float8_e4m3fn).view(np.uint8)
    else:
        c = by_word.astype(ml_dtypes.float4_e2m1fn).view(np.uint8) & 0xF
        words = (c[..., 0::2] | (c[..., 1::2] << 4)).reshape(k // 512, 128, 2 * n)
    return np.ascontiguousarray(words), np.ascontiguousarray(byte.astype(np.uint8).reshape(k // 512, 16, n))


def unpack_weight(words, scales, fmt):
    g, _, n = scales.shape
    words = np.ascontiguousarray(words).reshape(g, 128, n, -1)
    if fmt == "e4m3":
        vals = words.view(ml_dtypes.float8_e4m3fn).astype(np.float64)
    else:
        nib = np.empty((g, 128, n, 4), np.uint8)
        nib[..., 0::2] = words & 0xF
        nib[..., 1::2] = words >> 4
        vals = E2M1[nib]
    vals = vals * np.repeat(np.exp2(scales.astype(np.float64) - 127.0), 8, axis=1)[..., None]
    return vals.transpose(0, 1, 3, 2).reshape(g * 512, n)


def gelu(v):
    return 0.5 * v * (1.0 + np.tanh(np.sqrt(2.0 / np.pi) * (v + 0.044715 * v**3)))


def bf(x):
    return np.asarray(x, np.float32).astype(ml_dtypes.bfloat16)


def planes(Y):
    n, m = Y.shape
    b = f64(bf(Y)).reshape(n // 32, 32, m)
    amax = np.abs(b).max(1)
    byte = np.clip(np.where(amax > 0, np.frexp(amax)[1] - 1 + 127 - 7, 1), 1, 254)
    codes = (b * np.exp2(127.0 - byte)[:, None, :]).reshape(n, m).astype(np.float32).astype(ml_dtypes.float8_e4m3fn).view(np.uint8)
    words = codes.reshape(n // 512, 128, 4, m).transpose(0, 1, 3, 2)
    return np.ascontiguousarray(words), np.ascontiguousarray(byte.astype(np.uint8).reshape(n // 512, 16, m))


T, S, T2, P, K, K2, L, H, N = 2048, 512, 2048, 1024, 1024, 512, 512, 1024, 512

def setup_inputs():
    n = np.random.standard_normal
    s, s2 = mx_kscale(K)[:, None], mx_kscale(K2)[:, None]
    s3, u = mx_kscale(L)[:, None], mx_kscale(H)[:, None]
    size = np.exp(0.8 * n(N))
    perm = np.random.permutation(T2)
    d = {}
    d["tab_words"], d["tab_scales"] = pack_weight(n((K, T)) * s, "e4m3")
    d["tab2_words"], d["tab2_scales"] = pack_weight(n((K2, T)) * s2, "e4m3")
    d["offs"] = striped(np.random.permutation(T)[:S])
    d["offs2"] = striped(np.random.permutation(T)[:S])
    d["offs3"] = striped(perm[:S])
    d["offs4"] = striped(perm[S:2 * S])
    d["offs5"] = striped(np.random.permutation(T2)[:P])
    d["w1"] = (1.8 * n((K, H)) / s / K**0.5).astype(np.float32)
    d["w2_words"], d["w2_scales"] = pack_weight(0.8 * n((K, H)) / s / K**0.5, "e2m1")
    d["w3"] = (1.2 * n((K2, H)) / s2 / K2**0.5).astype(np.float32)
    d["cal"] = np.exp(0.5 * n(H)).astype(np.float32)
    d["page0"] = (1.3 * n((H, T2))).astype(np.float32)
    d["wg1"] = np.exp(0.3 * n((128, S))).astype(np.float32)
    d["wg2"] = np.exp(0.3 * n((128, S))).astype(np.float32)
    d["gain"] = (np.exp(0.3 * n(H)) * u[:, 0]).astype(np.float32)
    d["w4_words"], d["w4_scales"] = pack_weight(1.6 * n((H, N)) * size / u / H**0.5, "e4m3")
    d["w5"] = (0.9 * n((L, N)) * size / s3 / L**0.5).astype(np.float32)
    d["tide"] = (n((L, P)) * s3).astype(np.float32)
    return d

def reference(tab_words, tab_scales, tab2_words, tab2_scales, offs, offs2, offs3, offs4, offs5, w1, w2_words, w2_scales, w3, cal, page0, wg1, wg2, gain, w4_words, w4_scales, w5, tide):
    v = unpack_weight(tab_words, tab_scales, "e4m3")[:, unstriped(offs)]
    v2 = unpack_weight(tab2_words, tab2_scales, "e4m3")[:, unstriped(offs2)]
    b = mxq(f64(w1), 0, "e4m3").T @ v
    h1 = b / (1.0 + np.exp(-b)) + (unpack_weight(w2_words, w2_scales, "e2m1").T @ v)
    h2 = f64(cal)[:, None] * (mxq(f64(w3), 0, "e4m3").T @ v2)
    page = f64(page0).copy()
    page[:, unstriped(offs3)] = np.tile(f64(wg1), (H // 128, 1)) * h1
    page[:, unstriped(offs4)] = np.tile(f64(wg2), (H // 128, 1)) * h2
    x = mxq(f64(gain)[:, None] * np.tanh(page[:, unstriped(offs5)]), 0, "e4m3")
    e = unpack_weight(w4_words, w4_scales, "e4m3").T @ x
    f = mxq(f64(w5), 0, "e4m3").T @ mxq(f64(tide), 0, "e4m3")
    y = np.abs(e - f)
    words, scales = planes(y)
    return y, words, scales

@@ -1,0 +1,376 @@
+from contextlib import ExitStack
+
+import concourse.mybir as mybir
+from concourse.masks import make_identity
+
+F32 = mybir.dt.float32
+BF16 = mybir.dt.bfloat16
+I32 = mybir.dt.int32
+U32 = mybir.dt.uint32
+U16 = mybir.dt.uint16
+U8 = mybir.dt.uint8
+FP8X4 = mybir.dt.float8_e4m3fn_x4
+FP4X4 = mybir.dt.float4_e2m1fn_x4
+ACT = mybir.ActivationFunctionType
+MULT = mybir.AluOpType.mult
+
+FLOPS = 4294967296
+
+P = 128
+PACK = 4
+KP = P * PACK
+T = 2048
+S = 512
+J = 1024
+QW = 256
+NQ = J // QW
+
+
+def tile_list_oyster_raft_register_kernel(
+    tc, tab_words, tab_scales, tab2_words, tab2_scales, offs, offs2, offs3, offs4, offs5,
+    w1, w2_words, w2_scales, w3, cal, page0, wg1, wg2, gain, w4_words, w4_scales, w5, tide,
+    out_0, out_1, out_2,
+):
+    nc = tc.nc
+    with ExitStack() as ctx:
+        sb = ctx.enter_context(tc.tile_pool(name="sb", bufs=1))
+        hp = ctx.enter_context(tc.tile_pool(name="hp", bufs=1))
+        ps = ctx.enter_context(tc.psum_pool(name="ps", bufs=1))
+
+        def alloc(name, shape, dtype, tag=None, bufs=1):
+            return sb.tile(shape, dtype, name=name, tag=tag or name, bufs=bufs, align_bytes=64)
+
+        def alloc_big(name):
+            return alloc(name, [P, T], F32, tag="big", bufs=7)
+
+        idx = alloc("idx", [P, S // 16], U16)
+        idx2 = alloc("idx2", [P, S // 16], U16)
+        idx3 = alloc("idx3", [P, S // 16], U16)
+        idx4 = alloc("idx4", [P, S // 16], U16)
+        idx5 = alloc("idx5", [P, J // 16], U16)
+        pages = [alloc_big("page%d" % k) for k in range(6)]
+        tabw = [alloc("tabw%d" % a, [P, T], I32) for a in range(2)]
+        tabs = alloc("tabs", [P, 2, T], U8)
+        tab2w = alloc("tab2w", [P, T], I32)
+        tab2s = alloc("tab2s", [P, T], U8)
+        vw = [alloc("vw%d" % a, [P, S], U32) for a in range(2)]
+        vs = [alloc("vs%d" % a, [P, S], U8) for a in range(2)]
+        v2w = alloc("v2w", [P, S], U32)
+        v2s = alloc("v2s", [P, S], U8)
+        raw = [alloc("raw%d" % k, [P, 2048], F32) for k in range(3)]
+        stg = [alloc("stg%d" % k, [P, 2048], BF16) for k in range(5)]
+        w1c = [alloc("w1c%d" % a, [P, KP], U32) for a in range(2)]
+        w1s = [alloc("w1s%d" % a, [P, KP], U8) for a in range(2)]
+        w3c = alloc("w3c", [P, KP], U32)
+        w3s = alloc("w3s", [P, KP], U8)
+        w5c = alloc("w5c", [P, KP], U32)
+        w5s = alloc("w5s", [P, KP], U8)
+        tdc = alloc("tdc", [P, J], U32)
+        tds = alloc("tds", [P, J], U8)
+        xc = [alloc("xc%d" % b, [P, J], U32) for b in range(2)]
+        xs = [alloc("xs%d" % b, [P, J], U8) for b in range(2)]
+        yc = alloc("yc", [P, J], U32)
+        ys = alloc("ys", [P, J], U8)
+        w2w = [alloc("w2w%d" % b, [P, 2, 2 * KP], U8) for b in range(2)]
+        w2s = alloc("w2s", [P, 2, 2 * KP], U8)
+        w4w_raw = alloc("w4w_raw", [P, 2 * KP], I32)
+        w4s_raw = alloc("w4s_raw", [P, KP], U8)
+        wg_raw = [alloc("wg_raw%d" % k, [P, S], F32) for k in range(2)]
+        wgd = [alloc("wgd%d" % k, [P, PACK * S], F32) for k in range(2)]
+        w1_second = hp.tile([P, 4 * S], F32, name="w1_second", align_bytes=64, offset=2 * 8 * S)[:]
+        hh = [hp.tile([P, 2 * S], F32, name="hh%d" % t, align_bytes=64, offset=8 * S * t)[:] for t in range(PACK)]
+        xb = alloc("xb", [P, PACK, J], BF16)
+        ident = alloc("ident", [P, P], F32)
+        cal_t = alloc("cal_t", [P, 2, PACK], F32)
+        gain_t = alloc("gain_t", [P, 2, PACK], F32)
+        warm = alloc("warm", [P, 1], F32)
+        banks = [ps.tile([P, S], F32, name="bank%d" % k) for k in range(8)]
+
+        page_rows = page0.rearrange("(b p t) c -> b t p c", b=2, t=PACK)
+
+        def load_rows(dst, src):
+            nc.sync.dma_start(out=dst.rearrange("p (j c) -> p j c", j=PACK), in_=src.rearrange("(p j) c -> p j c", j=PACK))
+
+        def load_page(k):
+            nc.sync.dma_start(out=pages[k][:], in_=page_rows[k // PACK, k % PACK])
+
+        def load_words(dst, src):
+            nc.sync.dma_start(out=dst[:], in_=src.rearrange("p n t -> p (n t)").bitcast(I32))
+
+        def load_w2_words(b):
+            nc.sync.dma_start(out=w2w[b][:].bitcast(I32),
+                              in_=w2_words[:, :, 2 * KP * b:2 * KP * (b + 1)].rearrange("a p c -> p a c").bitcast(I32))
+
+        def copy(eng, out, in_):
+            if eng == "v":
+                nc.vector.tensor_copy(out, in_)
+            else:
+                nc.scalar.copy(out, in_)
+
+        def cast_dealt_views(dst, src):
+            return (dst[:].rearrange("p (t m j) -> p m j t", t=PACK, j=PACK),
+                    src[:].rearrange("p (j m t) -> p m j t", t=PACK, j=PACK))
+
+        def weave(eng, dst, src):
+            copy(eng, dst.rearrange("p (c i t) -> p c t i", i=4, t=PACK), src.rearrange("p t (c i) -> p c t i", i=4))
+
+        def quant(codes, scales, src):
+            nc.vector.quantize_mx(out=codes.bitcast(FP8X4), scales=scales, in_=src)
+
+        def mm(out, lc, ls, rc, rs, start, stop):
+            nc.tensor.matmul_mx(out=out, lhsT=lc, lhsT_scale=ls, rhs=rc, rhs_scale=rs, start=start, stop=stop)
+
+        def deal_wg(k, turn_bank, reps, out_banks):
+            for jt in range(4):
+                nc.tensor.transpose(turn_bank[:, P * jt:P * (jt + 1)], wg_raw[k][:, P * jt:P * (jt + 1)], ident[:])
+            turned = turn_bank[:].rearrange("p (jt q t) -> p t jt q", jt=4, t=PACK)
+            for t in range(PACK):
+                nc.scalar.copy(reps[t].rearrange("p (jt r q) -> p jt r q", jt=4, r=4),
+                               turned[:, t].unsqueeze(2).to_broadcast([P, 4, 4, 32]))
+            for t in range(PACK):
+                for jt in range(4):
+                    nc.tensor.transpose(out_banks[t][:, P * jt:P * (jt + 1)], reps[t][:, P * jt:P * (jt + 1)], ident[:])
+                nc.scalar.copy(wgd[k][:, S * t:S * (t + 1)], out_banks[t][:])
+
+        def rows_view(src):
+            return src.rearrange("p (j c) -> p j c", j=PACK)
+
+        def quant_w3(cast_eng, src):
+            dst, src = cast_dealt_views(stg[0], src)
+            copy(cast_eng, dst, src)
+            quant(w3c[:], w3s[:], stg[0][:])
+
+        def make_h2(b, t):
+            cols = slice(P * t, P * (t + 1))
+            bank = banks[6 + t % 2]
+            mm(bank[:], w3c[:, cols].bitcast(FP8X4), w3s[:, cols], v2w[:].bitcast(FP8X4), v2s[:], True, True)
+            nc.scalar.activation(hh[t][:, 0:S], bank[:], ACT.Copy, scale=cal_t[:, b, t:t + 1])
+
+        def quant_w1(cast_eng, a, src):
+            weave(cast_eng, stg[1 + a][:], rows_view(src))
+            quant(w1c[a][:], w1s[a][:], stg[1 + a][:])
+
+        silu_stage = [stg[0][:].bitcast(F32)[:, 0:S], raw[2][:, 0:S], raw[0][:, 0:S], raw[1][:, 0:S]]
+        lin_stage = [raw[2][:, 2 * S:3 * S], raw[2][:, 3 * S:4 * S]]
+
+        def turn_into_h1(jt, part, first, last):
+            for t in range(PACK):
+                nc.tensor.matmul(banks[t][:, P * jt:P * (jt + 1)], part[:, P * t:P * (t + 1)], ident[:],
+                                 start=first, stop=last, is_transpose=True)
+
+        def make_lin(b):
+            for jt in range(4):
+                cols = slice(P * jt, P * (jt + 1))
+                bank = banks[6 + jt % 2]
+                for a in range(2):
+                    mm(bank[:], vw[a][:, cols].bitcast(FP8X4), vs[a][:, cols],
+                       w2w[b][:, a, :].bitcast(FP4X4), w2s[:, a, KP * b:KP * (b + 1)], a == 0, a == 1)
+                part = lin_stage[jt % 2]
+                nc.scalar.copy(part.rearrange("p (t q) -> p t q", t=PACK), bank[:].rearrange("p (q t) -> p t q", t=PACK))
+                turn_into_h1(jt, part, jt == 0, False)
+
+        def make_silu(b):
+            for pair in range(2):
+                for jt in (2 * pair, 2 * pair + 1):
+                    cols = slice(P * jt, P * (jt + 1))
+                    bank = banks[4 + jt % 2]
+                    for a in range(2):
+                        mm(bank[:], vw[a][:, cols].bitcast(FP8X4), vs[a][:, cols],
+                           w1c[a][:].bitcast(FP8X4), w1s[a][:], a == 0, a == 1)
+                    nc.scalar.activation(silu_stage[jt].rearrange("p (t q) -> p t q", t=PACK),
+                                         bank[:].rearrange("p (q t) -> p t q", t=PACK), ACT.Silu)
+            for jt in range(4):
+                turn_into_h1(jt, silu_stage[jt], False, jt == 3)
+
+        def fetch_h1(t):
+            nc.scalar.copy(hh[t][:, S:2 * S], banks[t][:])
+
+        def put_h2(b, t):
+            nc.vector.tensor_tensor(pages[PACK * b + t][:].indirect(idx4[:]), hh[t][:, 0:S], wgd[1][:, S * t:S * (t + 1)], MULT)
+
+        def put_h1(b, t):
+            nc.vector.tensor_tensor(pages[PACK * b + t][:].indirect(idx3[:]), hh[t][:, S:2 * S], wgd[0][:, S * t:S * (t + 1)], MULT)
+
+        make_identity(nc, ident[:])
+        for plane in (tab2s, tabs, w2s, w4s_raw):
+            nc.vector.memset(plane[:].bitcast(I32), 0)
+
+        nc.sync.dma_start(idx2[:], offs2)
+        nc.sync.dma_start(idx[:], offs)
+        nc.sync.dma_start(idx4[:], offs4)
+        nc.sync.dma_start(out=cal_t[:], in_=cal.rearrange("(b p t) -> p b t", b=2, t=PACK))
+        nc.sync.dma_start(out=wg_raw[1][:], in_=wg2)
+        nc.sync.dma_start(out=wg_raw[0][:], in_=wg1)
+        load_rows(raw[0][:], w3[:, 0:KP])
+        load_words(tab2w, tab2_words[0])
+        for q in range(4):
+            nc.sync.dma_start(out=tab2s[32 * q:32 * q + 4, :].bitcast(I32), in_=tab2_scales[0, 4 * q:4 * q + 4, :].bitcast(I32))
+        nc.scalar.activation(warm[:], ident[:, 0:1], ACT.Silu)
+        load_words(tabw[0], tab_words[0])
+        for q in range(4):
+            nc.sync.dma_start(out=tabs[32 * q:32 * q + 4, :, :].bitcast(I32),
+                              in_=tab_scales[:, 4 * q:4 * q + 4, :].rearrange("a r t -> r a t").bitcast(I32))
+        load_words(tabw[1], tab_words[1])
+        load_page(0)
+        load_w2_words(0)
+        for q in range(4):
+            nc.sync.dma_start(out=w2s[32 * q:32 * q + 4, :, :].bitcast(I32),
+                              in_=w2_scales[:, 4 * q:4 * q + 4, :].rearrange("a r t -> r a t").bitcast(I32))
+        load_page(1)
+        load_rows(raw[1][:], w1[0:KP, 0:KP])
+        load_rows(w1_second, w1[KP:2 * KP, 0:KP])
+        load_page(2)
+        nc.sync.dma_start(idx3[:], offs3)
+        load_page(3)
+        nc.sync.dma_start(idx5[:], offs5)
+        nc.sync.dma_start(out=gain_t[:], in_=gain.rearrange("(b p t) -> p b t", b=2, t=PACK))
+        load_w2_words(1)
+
+        deal_wg(1, banks[7], [raw[2][:, S * t:S * (t + 1)] for t in range(PACK)], banks[0:4])
+        deal_wg(0, banks[6], [stg[1 + t // 2][:].bitcast(F32)[:, S * (t % 2):S * (t % 2 + 1)] for t in range(PACK)],
+                [banks[4], banks[5], banks[0], banks[1]])
+        quant_w3("v", raw[0])
+        nc.vector.tensor_copy(v2w[:], tab2w[:].bitcast(U32).indirect(idx2[:]))
+        nc.vector.tensor_copy(v2s[:], tab2s[:].indirect(idx2[:]))
+        nc.vector.tensor_copy(vw[0][:], tabw[0][:].bitcast(U32).indirect(idx[:]))
+        for a in range(2):
+            nc.vector.tensor_copy(vs[a][:], tabs[:, a, :].indirect(idx[:]))
+        nc.vector.tensor_copy(vw[1][:], tabw[1][:].bitcast(U32).indirect(idx[:]))
+        for t in range(2):
+            make_h2(0, t)
+            put_h2(0, t)
+        make_lin(0)
+        quant_w1("v", 0, raw[1][:])
+        quant_w1("s", 1, w1_second)
+        for t in range(2, 4):
+            make_h2(0, t)
+            put_h2(0, t)
+        make_silu(0)
+        for t in range(PACK):
+            fetch_h1(t)
+
+        load_rows(raw[2][:], w3[:, KP:2 * KP])
+        load_rows(raw[0][:], w1[KP:2 * KP, KP:2 * KP])
+        load_rows(raw[1][:], w1[0:KP, KP:2 * KP])
+        load_page(4)
+        load_page(5)
+        nc.sync.dma_start(out=w4w_raw[:].rearrange("p (a c) -> p a c", a=2),
+                          in_=w4_words.rearrange("a p c t -> p a (c t)").bitcast(I32))
+        for q in range(4):
+            nc.sync.dma_start(out=w4s_raw[32 * q:32 * q + 8, :].bitcast(I32), in_=w4_scales[:, 4 * q:4 * q + 4, :].bitcast(I32))
+
+        def read_page(t):
+            nc.vector.tensor_copy(hh[t], pages[t][:].indirect(idx5[:]))
+            bent = raw[1][:, J * (t % 2):J * (t % 2 + 1)]
+            nc.scalar.activation(bent, hh[t], ACT.Tanh)
+            nc.scalar.activation(xb[:, t, :], bent, ACT.Copy, scale=gain_t[:, 0, t:t + 1])
+
+        quant_w3("s", raw[2])
+        quant_w1("s", 1, raw[0][:])
+        quant_w1("s", 0, raw[1][:])
+        make_lin(1)
+        for t in range(3):
+            put_h1(0, t)
+            read_page(t)
+        put_h1(0, 3)
+        for t in range(2):
+            make_h2(1, t)
+        read_page(3)
+        for t in range(2, 4):
+            make_h2(1, t)
+        for k in range(6, 8):
+            pages.append(alloc_big("page%d" % k))
+            load_page(k)
+        tide_raw = [alloc_big("tide_raw%d" % h) for h in range(2)]
+        w5_raw = alloc_big("w5_raw")
+        for h in range(2):
+            load_rows(tide_raw[h][:], tide[:, KP * h:KP * (h + 1)])
+        load_rows(w5_raw[:], w5)
+        for t in range(PACK):
+            put_h2(1, t)
+        make_silu(1)
+        for t in range(2):
+            fetch_h1(t)
+        for h in range(2):
+            cols = slice(KP * h, KP * (h + 1))
+            weave("s", stg[1 + h][:], rows_view(tide_raw[h][:]))
+            quant(tdc[:, cols], tds[:, cols], stg[1 + h][:])
+        dst, src = cast_dealt_views(stg[0], w5_raw)
+        nc.scalar.activation(dst, src, ACT.Copy, scale=-1.0)
+        quant(w5c[:], w5s[:], stg[0][:])
+        for h in range(2):
+            cols = slice(KP * h, KP * (h + 1))
+            weave("s", stg[3 + h][:], xb[:, :, cols])
+            quant(xc[0][:, cols], xs[0][:, cols], stg[3 + h][:])
+        fetch_h1(2)
+        w4w = [alloc("w4w%d" % a, [P, KP], I32, tag="w1c%d" % a) for a in range(2)]
+        w4s = alloc("w4s", [P, KP], U8, tag="w1s0")
+        for a in range(2):
+            nc.vector.tensor_copy(w4w[a][:].rearrange("p (t q) -> p q t", t=PACK),
+                                  w4w_raw[:, KP * a:KP * (a + 1)].rearrange("p (q t) -> p q t", t=PACK))
+        nc.vector.tensor_copy(w4s[:].rearrange("p (t q) -> p q t", t=PACK), w4s_raw[:].rearrange("p (q t) -> p q t", t=PACK))
+        for t in range(PACK):
+            put_h1(1, t)
+            if t < PACK - 1:
+                nc.vector.tensor_copy(hh[t], pages[PACK + t][:].indirect(idx5[:]))
+                nc.scalar.activation(hh[t], hh[t], ACT.Tanh)
+                nc.scalar.activation(xb[:, t, :], hh[t], ACT.Copy, scale=gain_t[:, 1, t:t + 1])
+            if t == 1:
+                fetch_h1(3)
+
+        def e_pass(jq, t, a, stop):
+            cols = slice(QW * jq, QW * (jq + 1))
+            out = banks[2 * jq + t // 2][:, QW * (t % 2):QW * (t % 2 + 1)]
+            mm(out, w4w[a][:, P * t:P * (t + 1)].bitcast(FP8X4), w4s[4 * a:P, P * t:P * (t + 1)],
+               xc[a][:, cols].bitcast(FP8X4), xs[a][:, cols], False, stop)
+
+        for jq in range(NQ):
+            cols = slice(QW * jq, QW * (jq + 1))
+            for t in range(PACK):
+                out = banks[2 * jq + t // 2][:, QW * (t % 2):QW * (t % 2 + 1)]
+                mm(out, w5c[:, P * t:P * (t + 1)].bitcast(FP8X4), w5s[:, P * t:P * (t + 1)],
+                   tdc[:, cols].bitcast(FP8X4), tds[:, cols], t % 2 == 0, False)
+        for jq in range(NQ):
+            for t in range(PACK):
+                e_pass(jq, t, 0, False)
+
+        y_rows = out_0.rearrange("(p t) j -> p t j", t=PACK)
+        y_words = out_1[0].rearrange("p m t -> p (m t)").bitcast(I32)
+
+        def make_x(jq):
+            cols = slice(QW * jq, QW * (jq + 1))
+            last = PACK - 1
+            got = hh[last][:, cols]
+            nc.vector.tensor_copy(got, pages[PACK + last][:].indirect(idx5[:, 16 * jq:16 * (jq + 1)]))
+            nc.scalar.activation(got, got, ACT.Tanh)
+            nc.scalar.activation(xb[:, last, cols], got, ACT.Copy, scale=gain_t[:, 1, last:last + 1])
+
+        def make_y(jq):
+            cols = slice(QW * jq, QW * (jq + 1))
+            woven = stg[1 + jq // 2][:, J * (jq % 2):J * (jq % 2 + 1)]
+            weave("v", woven, xb[:, :, cols])
+            quant(xc[1][:, cols], xs[1][:, cols], woven)
+            y = raw[jq // 2][:, J * (jq % 2):J * (jq % 2 + 1)]
+            for t in range(PACK):
+                e_pass(jq, t, 1, t % 2 == 1)
+            for th in range(2):
+                nc.scalar.activation(y[:, S * th:S * (th + 1)], banks[2 * jq + th][:], ACT.Abs)
+            nc.sync.dma_start(out=y_rows[:, :, cols], in_=y.rearrange("p (t j) -> p t j", t=PACK))
+
+        def make_planes(jq):
+            cols = slice(QW * jq, QW * (jq + 1))
+            woven = stg[3 + jq // 2][:, J * (jq % 2):J * (jq % 2 + 1)]
+            y = raw[jq // 2][:, J * (jq % 2):J * (jq % 2 + 1)]
+            weave("v", woven, y.rearrange("p (t j) -> p t j", t=PACK))
+            quant(yc[:, cols], ys[:, cols], woven)
+            nc.sync.dma_start(out=y_words[:, cols], in_=yc[:, cols].bitcast(I32))
+
+        for jq in range(NQ):
+            make_x(jq)
+        for step in range(NQ + 1):
+            if step < NQ:
+                make_y(step)
+            if step >= 1:
+                make_planes(step - 1)
+        for q in range(4):
+            nc.sync.dma_start(out=out_2[0, 4 * q:4 * q + 4, :].bitcast(I32), in_=ys[32 * q:32 * q + 4, :].bitcast(I32))

@@ -34,7 +34,6 @@ def tile_list_oyster_raft_register_kernel(
     nc = tc.nc
     with ExitStack() as ctx:
         sb = ctx.enter_context(tc.tile_pool(name="sb", bufs=1))
-        hp = ctx.enter_context(tc.tile_pool(name="hp", bufs=1))
         ps = ctx.enter_context(tc.psum_pool(name="ps", bufs=1))
 
         def alloc(name, shape, dtype, tag=None, bufs=1):
@@ -48,6 +47,7 @@ def tile_list_oyster_raft_register_kernel(
         idx3 = alloc("idx3", [P, S // 16], U16)
         idx4 = alloc("idx4", [P, S // 16], U16)
         idx5 = alloc("idx5", [P, J // 16], U16)
+        w1_second = alloc_big("w1_second")[:]
         pages = [alloc_big("page%d" % k) for k in range(6)]
         tabw = [alloc("tabw%d" % a, [P, T], I32) for a in range(2)]
         tabs = alloc("tabs", [P, 2, T], U8)
@@ -77,8 +77,7 @@ def tile_list_oyster_raft_register_kernel(
         w4s_raw = alloc("w4s_raw", [P, KP], U8)
         wg_raw = [alloc("wg_raw%d" % k, [P, S], F32) for k in range(2)]
         wgd = [alloc("wgd%d" % k, [P, PACK * S], F32) for k in range(2)]
-        w1_second = hp.tile([P, 4 * S], F32, name="w1_second", align_bytes=64, offset=2 * 8 * S)[:]
-        hh = [hp.tile([P, 2 * S], F32, name="hh%d" % t, align_bytes=64, offset=8 * S * t)[:] for t in range(PACK)]
+        hh = [alloc("hh%d" % t, [P, 2 * S], F32)[:] for t in range(PACK)]
         xb = alloc("xb", [P, PACK, J], BF16)
         ident = alloc("ident", [P, P], F32)
         cal_t = alloc("cal_t", [P, 2, PACK], F32)
@@ -142,7 +141,7 @@ def tile_list_oyster_raft_register_kernel(
 
         def make_h2(b, t):
             cols = slice(P * t, P * (t + 1))
-            bank = banks[6 + t % 2]
+            bank = banks[4 + t % 2]
             mm(bank[:], w3c[:, cols].bitcast(FP8X4), w3s[:, cols], v2w[:].bitcast(FP8X4), v2s[:], True, True)
             nc.scalar.activation(hh[t][:, 0:S], bank[:], ACT.Copy, scale=cal_t[:, b, t:t + 1])
 
@@ -151,7 +150,7 @@ def tile_list_oyster_raft_register_kernel(
             quant(w1c[a][:], w1s[a][:], stg[1 + a][:])
 
         silu_stage = [stg[0][:].bitcast(F32)[:, 0:S], raw[2][:, 0:S], raw[0][:, 0:S], raw[1][:, 0:S]]
-        lin_stage = [raw[2][:, 2 * S:3 * S], raw[2][:, 3 * S:4 * S]]
+        lin_stage = [raw[2][:, S * jt:S * (jt + 1)] for jt in range(4)]
 
         def turn_into_h1(jt, part, first, last):
             for t in range(PACK):
@@ -161,25 +160,23 @@ def tile_list_oyster_raft_register_kernel(
         def make_lin(b):
             for jt in range(4):
                 cols = slice(P * jt, P * (jt + 1))
-                bank = banks[6 + jt % 2]
                 for a in range(2):
-                    mm(bank[:], vw[a][:, cols].bitcast(FP8X4), vs[a][:, cols],
+                    mm(banks[4 + jt][:], vw[a][:, cols].bitcast(FP8X4), vs[a][:, cols],
                        w2w[b][:, a, :].bitcast(FP4X4), w2s[:, a, KP * b:KP * (b + 1)], a == 0, a == 1)
-                part = lin_stage[jt % 2]
-                nc.scalar.copy(part.rearrange("p (t q) -> p t q", t=PACK), bank[:].rearrange("p (q t) -> p t q", t=PACK))
-                turn_into_h1(jt, part, jt == 0, False)
+            for jt in range(4):
+                nc.scalar.copy(lin_stage[jt].rearrange("p (t q) -> p t q", t=PACK),
+                               banks[4 + jt][:].rearrange("p (q t) -> p t q", t=PACK))
+                turn_into_h1(jt, lin_stage[jt], jt == 0, False)
 
         def make_silu(b):
-            for pair in range(2):
-                for jt in (2 * pair, 2 * pair + 1):
+            for a in range(2):
+                for jt in range(4):
                     cols = slice(P * jt, P * (jt + 1))
-                    bank = banks[4 + jt % 2]
-                    for a in range(2):
-                        mm(bank[:], vw[a][:, cols].bitcast(FP8X4), vs[a][:, cols],
-                           w1c[a][:].bitcast(FP8X4), w1s[a][:], a == 0, a == 1)
-                    nc.scalar.activation(silu_stage[jt].rearrange("p (t q) -> p t q", t=PACK),
-                                         bank[:].rearrange("p (q t) -> p t q", t=PACK), ACT.Silu)
+                    mm(banks[4 + jt][:], vw[a][:, cols].bitcast(FP8X4), vs[a][:, cols],
+                       w1c[a][:].bitcast(FP8X4), w1s[a][:], a == 0, a == 1)
             for jt in range(4):
+                nc.scalar.activation(silu_stage[jt].rearrange("p (t q) -> p t q", t=PACK),
+                                     banks[4 + jt][:].rearrange("p (q t) -> p t q", t=PACK), ACT.Silu)
                 turn_into_h1(jt, silu_stage[jt], False, jt == 3)
 
         def fetch_h1(t):
@@ -196,22 +193,22 @@ def tile_list_oyster_raft_register_kernel(
             nc.vector.memset(plane[:].bitcast(I32), 0)
 
         nc.sync.dma_start(idx2[:], offs2)
-        nc.sync.dma_start(idx[:], offs)
-        nc.sync.dma_start(idx4[:], offs4)
-        nc.sync.dma_start(out=cal_t[:], in_=cal.rearrange("(b p t) -> p b t", b=2, t=PACK))
         nc.sync.dma_start(out=wg_raw[1][:], in_=wg2)
-        nc.sync.dma_start(out=wg_raw[0][:], in_=wg1)
-        load_rows(raw[0][:], w3[:, 0:KP])
-        load_words(tab2w, tab2_words[0])
         for q in range(4):
             nc.sync.dma_start(out=tab2s[32 * q:32 * q + 4, :].bitcast(I32), in_=tab2_scales[0, 4 * q:4 * q + 4, :].bitcast(I32))
         nc.scalar.activation(warm[:], ident[:, 0:1], ACT.Silu)
+        load_rows(raw[0][:], w3[:, 0:KP])
+        load_words(tab2w, tab2_words[0])
+        nc.sync.dma_start(out=cal_t[:], in_=cal.rearrange("(b p t) -> p b t", b=2, t=PACK))
+        nc.sync.dma_start(idx4[:], offs4)
+        load_page(0)
+        nc.sync.dma_start(idx[:], offs)
+        nc.sync.dma_start(out=wg_raw[0][:], in_=wg1)
         load_words(tabw[0], tab_words[0])
         for q in range(4):
             nc.sync.dma_start(out=tabs[32 * q:32 * q + 4, :, :].bitcast(I32),
                               in_=tab_scales[:, 4 * q:4 * q + 4, :].rearrange("a r t -> r a t").bitcast(I32))
         load_words(tabw[1], tab_words[1])
-        load_page(0)
         load_w2_words(0)
         for q in range(4):
             nc.sync.dma_start(out=w2s[32 * q:32 * q + 4, :, :].bitcast(I32),
@@ -227,23 +224,22 @@ def tile_list_oyster_raft_register_kernel(
         load_w2_words(1)
 
         deal_wg(1, banks[7], [raw[2][:, S * t:S * (t + 1)] for t in range(PACK)], banks[0:4])
-        deal_wg(0, banks[6], [stg[1 + t // 2][:].bitcast(F32)[:, S * (t % 2):S * (t % 2 + 1)] for t in range(PACK)],
-                [banks[4], banks[5], banks[0], banks[1]])
+        nc.vector.tensor_copy(v2s[:], tab2s[:].indirect(idx2[:]))
         quant_w3("v", raw[0])
         nc.vector.tensor_copy(v2w[:], tab2w[:].bitcast(U32).indirect(idx2[:]))
-        nc.vector.tensor_copy(v2s[:], tab2s[:].indirect(idx2[:]))
+        for t in range(PACK):
+            make_h2(0, t)
+        put_h2(0, 0)
+        deal_wg(0, banks[6], [stg[1 + t // 2][:].bitcast(F32)[:, S * (t % 2):S * (t % 2 + 1)] for t in range(PACK)], banks[0:4])
         nc.vector.tensor_copy(vw[0][:], tabw[0][:].bitcast(U32).indirect(idx[:]))
         for a in range(2):
             nc.vector.tensor_copy(vs[a][:], tabs[:, a, :].indirect(idx[:]))
         nc.vector.tensor_copy(vw[1][:], tabw[1][:].bitcast(U32).indirect(idx[:]))
-        for t in range(2):
-            make_h2(0, t)
-            put_h2(0, t)
         make_lin(0)
+        put_h2(0, 1)
         quant_w1("v", 0, raw[1][:])
-        quant_w1("s", 1, w1_second)
+        quant_w1("v", 1, w1_second)
         for t in range(2, 4):
-            make_h2(0, t)
             put_h2(0, t)
         make_silu(0)
         for t in range(PACK):
@@ -355,7 +351,8 @@ def tile_list_oyster_raft_register_kernel(
                 e_pass(jq, t, 1, t % 2 == 1)
             for th in range(2):
                 nc.scalar.activation(y[:, S * th:S * (th + 1)], banks[2 * jq + th][:], ACT.Abs)
-            nc.sync.dma_start(out=y_rows[:, :, cols], in_=y.rearrange("p (t j) -> p t j", t=PACK))
+                nc.sync.dma_start(out=y_rows[:, 2 * th:2 * th + 2, cols],
+                                  in_=y[:, S * th:S * (th + 1)].rearrange("p (t j) -> p t j", t=2))
 
         def make_planes(jq):
             cols = slice(QW * jq, QW * (jq + 1))

@@ -47,7 +47,7 @@ def tile_list_oyster_raft_register_kernel(
         idx3 = alloc("idx3", [P, S // 16], U16)
         idx4 = alloc("idx4", [P, S // 16], U16)
         idx5 = alloc("idx5", [P, J // 16], U16)
-        w1_second = alloc_big("w1_second")[:]
+        w1_second = alloc("w1_second", [P, T], F32)[:]
         pages = [alloc_big("page%d" % k) for k in range(6)]
         tabw = [alloc("tabw%d" % a, [P, T], I32) for a in range(2)]
         tabs = alloc("tabs", [P, 2, T], U8)
@@ -112,6 +112,10 @@ def tile_list_oyster_raft_register_kernel(
 
         def weave(eng, dst, src):
             copy(eng, dst.rearrange("p (c i t) -> p c t i", i=4, t=PACK), src.rearrange("p t (c i) -> p c t i", i=4))
+
+        def weave_pair(eng, dst, src, u):
+            copy(eng, dst.rearrange("p (c i u e) -> p u c e i", i=4, u=2, e=2)[:, u],
+                 src[:, 2 * u:2 * u + 2, :].rearrange("p e (c i) -> p c e i", i=4))
 
         def quant(codes, scales, src):
             nc.vector.quantize_mx(out=codes.bitcast(FP8X4), scales=scales, in_=src)
@@ -193,26 +197,26 @@ def tile_list_oyster_raft_register_kernel(
             nc.vector.memset(plane[:].bitcast(I32), 0)
 
         nc.sync.dma_start(idx2[:], offs2)
-        nc.sync.dma_start(out=wg_raw[1][:], in_=wg2)
-        for q in range(4):
-            nc.sync.dma_start(out=tab2s[32 * q:32 * q + 4, :].bitcast(I32), in_=tab2_scales[0, 4 * q:4 * q + 4, :].bitcast(I32))
-        nc.scalar.activation(warm[:], ident[:, 0:1], ACT.Silu)
-        load_rows(raw[0][:], w3[:, 0:KP])
-        load_words(tab2w, tab2_words[0])
         nc.sync.dma_start(out=cal_t[:], in_=cal.rearrange("(b p t) -> p b t", b=2, t=PACK))
         nc.sync.dma_start(idx4[:], offs4)
+        nc.sync.dma_start(out=wg_raw[1][:], in_=wg2)
+        load_rows(raw[0][:], w3[:, 0:KP])
+        for r in range(4):
+            nc.sync.dma_start(out=tab2s[r:P:32, :].bitcast(I32), in_=tab2_scales[0, r:16:4, :].bitcast(I32))
+        nc.scalar.activation(warm[:], ident[:, 0:1], ACT.Silu)
+        load_words(tab2w, tab2_words[0])
         load_page(0)
         nc.sync.dma_start(idx[:], offs)
         nc.sync.dma_start(out=wg_raw[0][:], in_=wg1)
         load_words(tabw[0], tab_words[0])
-        for q in range(4):
-            nc.sync.dma_start(out=tabs[32 * q:32 * q + 4, :, :].bitcast(I32),
-                              in_=tab_scales[:, 4 * q:4 * q + 4, :].rearrange("a r t -> r a t").bitcast(I32))
+        for r in range(4):
+            nc.sync.dma_start(out=tabs[r:P:32, :, :].bitcast(I32),
+                              in_=tab_scales[:, r:16:4, :].rearrange("a q t -> q a t").bitcast(I32))
         load_words(tabw[1], tab_words[1])
         load_w2_words(0)
-        for q in range(4):
-            nc.sync.dma_start(out=w2s[32 * q:32 * q + 4, :, :].bitcast(I32),
-                              in_=w2_scales[:, 4 * q:4 * q + 4, :].rearrange("a r t -> r a t").bitcast(I32))
+        for r in range(4):
+            nc.sync.dma_start(out=w2s[r:P:32, :, :].bitcast(I32),
+                              in_=w2_scales[:, r:16:4, :].rearrange("a q t -> q a t").bitcast(I32))
         load_page(1)
         load_rows(raw[1][:], w1[0:KP, 0:KP])
         load_rows(w1_second, w1[KP:2 * KP, 0:KP])
@@ -224,8 +228,8 @@ def tile_list_oyster_raft_register_kernel(
         load_w2_words(1)
 
         deal_wg(1, banks[7], [raw[2][:, S * t:S * (t + 1)] for t in range(PACK)], banks[0:4])
-        nc.vector.tensor_copy(v2s[:], tab2s[:].indirect(idx2[:]))
         quant_w3("v", raw[0])
+        nc.vector.tensor_copy(v2s[:], tab2s[:].indirect(idx2[:]))
         nc.vector.tensor_copy(v2w[:], tab2w[:].bitcast(U32).indirect(idx2[:]))
         for t in range(PACK):
             make_h2(0, t)
@@ -313,6 +317,8 @@ def tile_list_oyster_raft_register_kernel(
                 nc.scalar.activation(xb[:, t, :], hh[t], ACT.Copy, scale=gain_t[:, 1, t:t + 1])
             if t == 1:
                 fetch_h1(3)
+                for h in range(2):
+                    weave_pair("s", stg[1 + h][:], xb[:, :, KP * h:KP * (h + 1)], 0)
 
         def e_pass(jq, t, a, stop):
             cols = slice(QW * jq, QW * (jq + 1))
@@ -338,13 +344,14 @@ def tile_list_oyster_raft_register_kernel(
             last = PACK - 1
             got = hh[last][:, cols]
             nc.vector.tensor_copy(got, pages[PACK + last][:].indirect(idx5[:, 16 * jq:16 * (jq + 1)]))
-            nc.scalar.activation(got, got, ACT.Tanh)
-            nc.scalar.activation(xb[:, last, cols], got, ACT.Copy, scale=gain_t[:, 1, last:last + 1])
+            bent = hh[last - 1][:, cols]
+            nc.scalar.activation(bent, got, ACT.Tanh)
+            nc.scalar.activation(xb[:, last, cols], bent, ACT.Copy, scale=gain_t[:, 1, last:last + 1])
 
         def make_y(jq):
             cols = slice(QW * jq, QW * (jq + 1))
             woven = stg[1 + jq // 2][:, J * (jq % 2):J * (jq % 2 + 1)]
-            weave("v", woven, xb[:, :, cols])
+            weave_pair("v", woven, xb[:, :, cols], 1)
             quant(xc[1][:, cols], xs[1][:, cols], woven)
             y = raw[jq // 2][:, J * (jq % 2):J * (jq % 2 + 1)]
             for t in range(PACK):
@@ -369,5 +376,6 @@ def tile_list_oyster_raft_register_kernel(
                 make_y(step)
             if step >= 1:
                 make_planes(step - 1)
-        for q in range(4):
-            nc.sync.dma_start(out=out_2[0, 4 * q:4 * q + 4, :].bitcast(I32), in_=ys[32 * q:32 * q + 4, :].bitcast(I32))
+        for r in range(4):
+            queue = nc.sync if r % 2 == 0 else nc.scalar
+            queue.dma_start(out=out_2[0, r:16:4, :].bitcast(I32), in_=ys[r:P:32, :].bitcast(I32))

@@ -40,7 +40,7 @@ def tile_list_oyster_raft_register_kernel(
             return sb.tile(shape, dtype, name=name, tag=tag or name, bufs=bufs, align_bytes=64)
 
         def alloc_big(name):
-            return alloc(name, [P, T], F32, tag="big", bufs=7)
+            return alloc(name, [P, T], F32, tag="big", bufs=8)
 
         idx = alloc("idx", [P, S // 16], U16)
         idx2 = alloc("idx2", [P, S // 16], U16)
@@ -48,7 +48,7 @@ def tile_list_oyster_raft_register_kernel(
         idx4 = alloc("idx4", [P, S // 16], U16)
         idx5 = alloc("idx5", [P, J // 16], U16)
         w1_second = alloc("w1_second", [P, T], F32)[:]
-        pages = [alloc_big("page%d" % k) for k in range(6)]
+        pages = [alloc_big("page%d" % k) for k in range(8)]
         tabw = [alloc("tabw%d" % a, [P, T], I32) for a in range(2)]
         tabs = alloc("tabs", [P, 2, T], U8)
         tab2w = alloc("tab2w", [P, T], I32)
@@ -57,7 +57,8 @@ def tile_list_oyster_raft_register_kernel(
         vs = [alloc("vs%d" % a, [P, S], U8) for a in range(2)]
         v2w = alloc("v2w", [P, S], U32)
         v2s = alloc("v2s", [P, S], U8)
-        raw = [alloc("raw%d" % k, [P, 2048], F32) for k in range(3)]
+        h_all = alloc("h_all", [P, (PACK + 2) * 2 * S], F32)
+        raw = [alloc("raw0", [P, 2048], F32), h_all[:, PACK * 2 * S:(PACK + 2) * 2 * S], alloc("raw2", [P, 2048], F32)]
         stg = [alloc("stg%d" % k, [P, 2048], BF16) for k in range(5)]
         w1c = [alloc("w1c%d" % a, [P, KP], U32) for a in range(2)]
         w1s = [alloc("w1s%d" % a, [P, KP], U8) for a in range(2)]
@@ -75,9 +76,9 @@ def tile_list_oyster_raft_register_kernel(
         w2s = alloc("w2s", [P, 2, 2 * KP], U8)
         w4w_raw = alloc("w4w_raw", [P, 2 * KP], I32)
         w4s_raw = alloc("w4s_raw", [P, KP], U8)
-        wg_raw = [alloc("wg_raw%d" % k, [P, S], F32) for k in range(2)]
+        wg_raw = alloc("wg_raw", [P, S], F32)
         wgd = [alloc("wgd%d" % k, [P, PACK * S], F32) for k in range(2)]
-        hh = [alloc("hh%d" % t, [P, 2 * S], F32)[:] for t in range(PACK)]
+        hh = [h_all[:, 2 * S * t:2 * S * (t + 1)] for t in range(PACK)]
         xb = alloc("xb", [P, PACK, J], BF16)
         ident = alloc("ident", [P, P], F32)
         cal_t = alloc("cal_t", [P, 2, PACK], F32)
@@ -125,7 +126,7 @@ def tile_list_oyster_raft_register_kernel(
 
         def deal_wg(k, turn_bank, reps, out_banks):
             for jt in range(4):
-                nc.tensor.transpose(turn_bank[:, P * jt:P * (jt + 1)], wg_raw[k][:, P * jt:P * (jt + 1)], ident[:])
+                nc.tensor.transpose(turn_bank[:, P * jt:P * (jt + 1)], wg_raw[:, P * jt:P * (jt + 1)], ident[:])
             turned = turn_bank[:].rearrange("p (jt q t) -> p t jt q", jt=4, t=PACK)
             for t in range(PACK):
                 nc.scalar.copy(reps[t].rearrange("p (jt r q) -> p jt r q", jt=4, r=4),
@@ -153,7 +154,7 @@ def tile_list_oyster_raft_register_kernel(
             weave(cast_eng, stg[1 + a][:], rows_view(src))
             quant(w1c[a][:], w1s[a][:], stg[1 + a][:])
 
-        silu_stage = [stg[0][:].bitcast(F32)[:, 0:S], raw[2][:, 0:S], raw[0][:, 0:S], raw[1][:, 0:S]]
+        silu_stage = [w1_second[:, S * jt:S * (jt + 1)] for jt in range(4)]
         lin_stage = [raw[2][:, S * jt:S * (jt + 1)] for jt in range(4)]
 
         def turn_into_h1(jt, part, first, last):
@@ -199,105 +200,117 @@ def tile_list_oyster_raft_register_kernel(
         nc.sync.dma_start(idx2[:], offs2)
         nc.sync.dma_start(out=cal_t[:], in_=cal.rearrange("(b p t) -> p b t", b=2, t=PACK))
         nc.sync.dma_start(idx4[:], offs4)
-        nc.sync.dma_start(out=wg_raw[1][:], in_=wg2)
+        nc.sync.dma_start(out=wg_raw[:], in_=wg2)
         load_rows(raw[0][:], w3[:, 0:KP])
         for r in range(4):
             nc.sync.dma_start(out=tab2s[r:P:32, :].bitcast(I32), in_=tab2_scales[0, r:16:4, :].bitcast(I32))
         nc.scalar.activation(warm[:], ident[:, 0:1], ACT.Silu)
         load_words(tab2w, tab2_words[0])
         load_page(0)
+        load_page(1)
+        deal_wg(1, banks[7], [raw[2][:, S * t:S * (t + 1)] for t in range(PACK)], banks[0:4])
+        nc.sync.dma_start(out=wg_raw[:], in_=wg1)
         nc.sync.dma_start(idx[:], offs)
-        nc.sync.dma_start(out=wg_raw[0][:], in_=wg1)
         load_words(tabw[0], tab_words[0])
         for r in range(4):
             nc.sync.dma_start(out=tabs[r:P:32, :, :].bitcast(I32),
                               in_=tab_scales[:, r:16:4, :].rearrange("a q t -> q a t").bitcast(I32))
-        load_words(tabw[1], tab_words[1])
-        load_w2_words(0)
-        for r in range(4):
-            nc.sync.dma_start(out=w2s[r:P:32, :, :].bitcast(I32),
-                              in_=w2_scales[:, r:16:4, :].rearrange("a q t -> q a t").bitcast(I32))
-        load_page(1)
-        load_rows(raw[1][:], w1[0:KP, 0:KP])
-        load_rows(w1_second, w1[KP:2 * KP, 0:KP])
         load_page(2)
-        nc.sync.dma_start(idx3[:], offs3)
-        load_page(3)
-        nc.sync.dma_start(idx5[:], offs5)
-        nc.sync.dma_start(out=gain_t[:], in_=gain.rearrange("(b p t) -> p b t", b=2, t=PACK))
-        load_w2_words(1)
 
-        deal_wg(1, banks[7], [raw[2][:, S * t:S * (t + 1)] for t in range(PACK)], banks[0:4])
         quant_w3("v", raw[0])
         nc.vector.tensor_copy(v2s[:], tab2s[:].indirect(idx2[:]))
         nc.vector.tensor_copy(v2w[:], tab2w[:].bitcast(U32).indirect(idx2[:]))
         for t in range(PACK):
             make_h2(0, t)
-        put_h2(0, 0)
         deal_wg(0, banks[6], [stg[1 + t // 2][:].bitcast(F32)[:, S * (t % 2):S * (t % 2 + 1)] for t in range(PACK)], banks[0:4])
+        for t in range(2):
+            put_h2(0, t)
         nc.vector.tensor_copy(vw[0][:], tabw[0][:].bitcast(U32).indirect(idx[:]))
         for a in range(2):
             nc.vector.tensor_copy(vs[a][:], tabs[:, a, :].indirect(idx[:]))
+        put_h2(0, 2)
+
+        load_rows(raw[0][:], w3[:, KP:2 * KP])
+        load_page(3)
+        load_words(tabw[1], tab_words[1])
+        load_page(4)
+        load_w2_words(0)
+        for r in range(4):
+            nc.sync.dma_start(out=w2s[r:P:32, :, :].bitcast(I32),
+                              in_=w2_scales[:, r:16:4, :].rearrange("a q t -> q a t").bitcast(I32))
+        load_page(5)
+        load_rows(raw[1][:], w1[0:KP, 0:KP])
+        load_rows(w1_second, w1[KP:2 * KP, 0:KP])
+        load_page(6)
+        nc.sync.dma_start(idx3[:], offs3)
+        load_page(7)
+        nc.sync.dma_start(idx5[:], offs5)
+        nc.sync.dma_start(out=gain_t[:], in_=gain.rearrange("(b p t) -> p b t", b=2, t=PACK))
+        load_w2_words(1)
+
+        quant_w3("s", raw[0])
+        put_h2(0, 3)
         nc.vector.tensor_copy(vw[1][:], tabw[1][:].bitcast(U32).indirect(idx[:]))
-        make_lin(0)
-        put_h2(0, 1)
-        quant_w1("v", 0, raw[1][:])
-        quant_w1("v", 1, w1_second)
-        for t in range(2, 4):
-            put_h2(0, t)
-        make_silu(0)
         for t in range(PACK):
+            make_h2(1, t)
+        make_lin(0)
+        for t in range(2):
+            put_h2(1, t)
+        quant_w1("v", 0, raw[1][:])
+        quant_w1("s", 1, w1_second)
+        for t in range(2, 4):
+            put_h2(1, t)
+        make_silu(0)
+        for t in range(2):
             fetch_h1(t)
 
-        load_rows(raw[2][:], w3[:, KP:2 * KP])
-        load_rows(raw[0][:], w1[KP:2 * KP, KP:2 * KP])
+        w1_last = h_all[:, 2 * 2 * S:4 * 2 * S]
         load_rows(raw[1][:], w1[0:KP, KP:2 * KP])
-        load_page(4)
-        load_page(5)
+        load_rows(w1_last, w1[KP:2 * KP, KP:2 * KP])
         nc.sync.dma_start(out=w4w_raw[:].rearrange("p (a c) -> p a c", a=2),
                           in_=w4_words.rearrange("a p c t -> p a (c t)").bitcast(I32))
         for q in range(4):
             nc.sync.dma_start(out=w4s_raw[32 * q:32 * q + 8, :].bitcast(I32), in_=w4_scales[:, 4 * q:4 * q + 4, :].bitcast(I32))
+        load_rows(raw[0][:], w5)
 
         def read_page(t):
             nc.vector.tensor_copy(hh[t], pages[t][:].indirect(idx5[:]))
-            bent = raw[1][:, J * (t % 2):J * (t % 2 + 1)]
-            nc.scalar.activation(bent, hh[t], ACT.Tanh)
-            nc.scalar.activation(xb[:, t, :], bent, ACT.Copy, scale=gain_t[:, 0, t:t + 1])
+            if t < 2:
+                bent = h_all[:, 4 * S:12 * S].rearrange("p (u x) -> p u x", u=2)[:, :, 2 * S * t:2 * S * t + S]
+            else:
+                bent = raw[1].rearrange("p (u x) -> p u x", u=2)[:, :, S * (3 - t):S * (4 - t)]
+            nc.scalar.activation(bent, hh[t].rearrange("p (u x) -> p u x", u=2), ACT.Tanh)
+            nc.scalar.activation(xb[:, t, :].rearrange("p (u x) -> p u x", u=2), bent, ACT.Copy, scale=gain_t[:, 0, t:t + 1])
 
-        quant_w3("s", raw[2])
-        quant_w1("s", 1, raw[0][:])
         quant_w1("s", 0, raw[1][:])
+        quant_w1("s", 1, w1_last)
+        for t in range(2, 4):
+            fetch_h1(t)
         make_lin(1)
-        for t in range(3):
+        for t in range(2):
             put_h1(0, t)
             read_page(t)
-        put_h1(0, 3)
-        for t in range(2):
-            make_h2(1, t)
-        read_page(3)
-        for t in range(2, 4):
-            make_h2(1, t)
-        for k in range(6, 8):
-            pages.append(alloc_big("page%d" % k))
-            load_page(k)
         tide_raw = [alloc_big("tide_raw%d" % h) for h in range(2)]
-        w5_raw = alloc_big("w5_raw")
         for h in range(2):
             load_rows(tide_raw[h][:], tide[:, KP * h:KP * (h + 1)])
-        load_rows(w5_raw[:], w5)
-        for t in range(PACK):
-            put_h2(1, t)
-        make_silu(1)
-        for t in range(2):
-            fetch_h1(t)
-        for h in range(2):
+
+        def quant_tide(h):
             cols = slice(KP * h, KP * (h + 1))
             weave("s", stg[1 + h][:], rows_view(tide_raw[h][:]))
             quant(tdc[:, cols], tds[:, cols], stg[1 + h][:])
-        dst, src = cast_dealt_views(stg[0], w5_raw)
+
+        dst, src = cast_dealt_views(stg[0], raw[0])
         nc.scalar.activation(dst, src, ACT.Copy, scale=-1.0)
         quant(w5c[:], w5s[:], stg[0][:])
+        quant_tide(0)
+        make_silu(1)
+        for t in range(2):
+            fetch_h1(t)
+        quant_tide(1)
+        put_h1(0, 2)
+        read_page(2)
+        put_h1(0, 3)
+        read_page(3)
         for h in range(2):
             cols = slice(KP * h, KP * (h + 1))
             weave("s", stg[3 + h][:], xb[:, :, cols])

from contextlib import ExitStack

import concourse.mybir as mybir
from concourse.masks import make_identity

F32 = mybir.dt.float32
BF16 = mybir.dt.bfloat16
I32 = mybir.dt.int32
U32 = mybir.dt.uint32
U16 = mybir.dt.uint16
U8 = mybir.dt.uint8
FP8X4 = mybir.dt.float8_e4m3fn_x4
FP4X4 = mybir.dt.float4_e2m1fn_x4
ACT = mybir.ActivationFunctionType
MULT = mybir.AluOpType.mult

FLOPS = 4294967296

P = 128
PACK = 4
KP = P * PACK
T = 2048
S = 512
J = 1024
QW = 256
NQ = J // QW


def tile_list_oyster_raft_register_kernel(
    tc, tab_words, tab_scales, tab2_words, tab2_scales, offs, offs2, offs3, offs4, offs5,
    w1, w2_words, w2_scales, w3, cal, page0, wg1, wg2, gain, w4_words, w4_scales, w5, tide,
    out_0, out_1, out_2,
):
    nc = tc.nc
    with ExitStack() as ctx:
        sb = ctx.enter_context(tc.tile_pool(name="sb", bufs=1))
        ps = ctx.enter_context(tc.psum_pool(name="ps", bufs=1))

        def alloc(name, shape, dtype, tag=None, bufs=1):
            return sb.tile(shape, dtype, name=name, tag=tag or name, bufs=bufs, align_bytes=64)

        def alloc_big(name):
            return alloc(name, [P, T], F32, tag="big", bufs=8)

        idx = alloc("idx", [P, S // 16], U16)
        idx2 = alloc("idx2", [P, S // 16], U16)
        idx3 = alloc("idx3", [P, S // 16], U16)
        idx4 = alloc("idx4", [P, S // 16], U16)
        idx5 = alloc("idx5", [P, J // 16], U16)
        w1_second = alloc("w1_second", [P, T], F32)[:]
        pages = [alloc_big("page%d" % k) for k in range(8)]
        tabw = [alloc("tabw%d" % a, [P, T], I32) for a in range(2)]
        tabs = alloc("tabs", [P, 2, T], U8)
        tab2w = alloc("tab2w", [P, T], I32)
        tab2s = alloc("tab2s", [P, T], U8)
        vw = [alloc("vw%d" % a, [P, S], U32) for a in range(2)]
        vs = [alloc("vs%d" % a, [P, S], U8) for a in range(2)]
        v2w = alloc("v2w", [P, S], U32)
        v2s = alloc("v2s", [P, S], U8)
        h_all = alloc("h_all", [P, (PACK + 2) * 2 * S], F32)
        raw = [alloc("raw0", [P, 2048], F32), h_all[:, PACK * 2 * S:(PACK + 2) * 2 * S], alloc("raw2", [P, 2048], F32)]
        stg = [alloc("stg%d" % k, [P, 2048], BF16) for k in range(5)]
        w1c = [alloc("w1c%d" % a, [P, KP], U32) for a in range(2)]
        w1s = [alloc("w1s%d" % a, [P, KP], U8) for a in range(2)]
        w3c = alloc("w3c", [P, KP], U32)
        w3s = alloc("w3s", [P, KP], U8)
        w5c = alloc("w5c", [P, KP], U32)
        w5s = alloc("w5s", [P, KP], U8)
        tdc = alloc("tdc", [P, J], U32)
        tds = alloc("tds", [P, J], U8)
        xc = [alloc("xc%d" % b, [P, J], U32) for b in range(2)]
        xs = [alloc("xs%d" % b, [P, J], U8) for b in range(2)]
        yc = alloc("yc", [P, J], U32)
        ys = alloc("ys", [P, J], U8)
        w2w = [alloc("w2w%d" % b, [P, 2, 2 * KP], U8) for b in range(2)]
        w2s = alloc("w2s", [P, 2, 2 * KP], U8)
        w4w_raw = alloc("w4w_raw", [P, 2 * KP], I32)
        w4s_raw = alloc("w4s_raw", [P, KP], U8)
        wg_raw = alloc("wg_raw", [P, S], F32)
        wgd = [alloc("wgd%d" % k, [P, PACK * S], F32) for k in range(2)]
        hh = [h_all[:, 2 * S * t:2 * S * (t + 1)] for t in range(PACK)]
        xb = alloc("xb", [P, PACK, J], BF16)
        ident = alloc("ident", [P, P], F32)
        cal_t = alloc("cal_t", [P, 2, PACK], F32)
        gain_t = alloc("gain_t", [P, 2, PACK], F32)
        warm = alloc("warm", [P, 1], F32)
        banks = [ps.tile([P, S], F32, name="bank%d" % k) for k in range(8)]

        page_rows = page0.rearrange("(b p t) c -> b t p c", b=2, t=PACK)

        def load_rows(dst, src):
            nc.sync.dma_start(out=dst.rearrange("p (j c) -> p j c", j=PACK), in_=src.rearrange("(p j) c -> p j c", j=PACK))

        def load_page(k):
            nc.sync.dma_start(out=pages[k][:], in_=page_rows[k // PACK, k % PACK])

        def load_words(dst, src):
            nc.sync.dma_start(out=dst[:], in_=src.rearrange("p n t -> p (n t)").bitcast(I32))

        def load_w2_words(b):
            nc.sync.dma_start(out=w2w[b][:].bitcast(I32),
                              in_=w2_words[:, :, 2 * KP * b:2 * KP * (b + 1)].rearrange("a p c -> p a c").bitcast(I32))

        def copy(eng, out, in_):
            if eng == "v":
                nc.vector.tensor_copy(out, in_)
            else:
                nc.scalar.copy(out, in_)

        def cast_dealt_views(dst, src):
            return (dst[:].rearrange("p (t m j) -> p m j t", t=PACK, j=PACK),
                    src[:].rearrange("p (j m t) -> p m j t", t=PACK, j=PACK))

        def weave(eng, dst, src):
            copy(eng, dst.rearrange("p (c i t) -> p c t i", i=4, t=PACK), src.rearrange("p t (c i) -> p c t i", i=4))

        def weave_pair(eng, dst, src, u):
            copy(eng, dst.rearrange("p (c i u e) -> p u c e i", i=4, u=2, e=2)[:, u],
                 src[:, 2 * u:2 * u + 2, :].rearrange("p e (c i) -> p c e i", i=4))

        def quant(codes, scales, src):
            nc.vector.quantize_mx(out=codes.bitcast(FP8X4), scales=scales, in_=src)

        def mm(out, lc, ls, rc, rs, start, stop):
            nc.tensor.matmul_mx(out=out, lhsT=lc, lhsT_scale=ls, rhs=rc, rhs_scale=rs, start=start, stop=stop)

        def deal_wg(k, turn_bank, reps, out_banks):
            for jt in range(4):
                nc.tensor.transpose(turn_bank[:, P * jt:P * (jt + 1)], wg_raw[:, P * jt:P * (jt + 1)], ident[:])
            turned = turn_bank[:].rearrange("p (jt q t) -> p t jt q", jt=4, t=PACK)
            for t in range(PACK):
                nc.scalar.copy(reps[t].rearrange("p (jt r q) -> p jt r q", jt=4, r=4),
                               turned[:, t].unsqueeze(2).to_broadcast([P, 4, 4, 32]))
            for t in range(PACK):
                for jt in range(4):
                    nc.tensor.transpose(out_banks[t][:, P * jt:P * (jt + 1)], reps[t][:, P * jt:P * (jt + 1)], ident[:])
                nc.scalar.copy(wgd[k][:, S * t:S * (t + 1)], out_banks[t][:])

        def rows_view(src):
            return src.rearrange("p (j c) -> p j c", j=PACK)

        def quant_w3(cast_eng, src):
            dst, src = cast_dealt_views(stg[0], src)
            copy(cast_eng, dst, src)
            quant(w3c[:], w3s[:], stg[0][:])

        def make_h2(b, t):
            cols = slice(P * t, P * (t + 1))
            bank = banks[4 + t % 2]
            mm(bank[:], w3c[:, cols].bitcast(FP8X4), w3s[:, cols], v2w[:].bitcast(FP8X4), v2s[:], True, True)
            nc.scalar.activation(hh[t][:, 0:S], bank[:], ACT.Copy, scale=cal_t[:, b, t:t + 1])

        def quant_w1(cast_eng, a, src):
            weave(cast_eng, stg[1 + a][:], rows_view(src))
            quant(w1c[a][:], w1s[a][:], stg[1 + a][:])

        silu_stage = [w1_second[:, S * jt:S * (jt + 1)] for jt in range(4)]
        lin_stage = [raw[2][:, S * jt:S * (jt + 1)] for jt in range(4)]

        def turn_into_h1(jt, part, first, last):
            for t in range(PACK):
                nc.tensor.matmul(banks[t][:, P * jt:P * (jt + 1)], part[:, P * t:P * (t + 1)], ident[:],
                                 start=first, stop=last, is_transpose=True)

        def make_lin(b):
            for jt in range(4):
                cols = slice(P * jt, P * (jt + 1))
                for a in range(2):
                    mm(banks[4 + jt][:], vw[a][:, cols].bitcast(FP8X4), vs[a][:, cols],
                       w2w[b][:, a, :].bitcast(FP4X4), w2s[:, a, KP * b:KP * (b + 1)], a == 0, a == 1)
            for jt in range(4):
                nc.scalar.copy(lin_stage[jt].rearrange("p (t q) -> p t q", t=PACK),
                               banks[4 + jt][:].rearrange("p (q t) -> p t q", t=PACK))
                turn_into_h1(jt, lin_stage[jt], jt == 0, False)

        def make_silu(b):
            for a in range(2):
                for jt in range(4):
                    cols = slice(P * jt, P * (jt + 1))
                    mm(banks[4 + jt][:], vw[a][:, cols].bitcast(FP8X4), vs[a][:, cols],
                       w1c[a][:].bitcast(FP8X4), w1s[a][:], a == 0, a == 1)
            for jt in range(4):
                nc.scalar.activation(silu_stage[jt].rearrange("p (t q) -> p t q", t=PACK),
                                     banks[4 + jt][:].rearrange("p (q t) -> p t q", t=PACK), ACT.Silu)
                turn_into_h1(jt, silu_stage[jt], False, jt == 3)

        def fetch_h1(t):
            nc.scalar.copy(hh[t][:, S:2 * S], banks[t][:])

        def put_h2(b, t):
            nc.vector.tensor_tensor(pages[PACK * b + t][:].indirect(idx4[:]), hh[t][:, 0:S], wgd[1][:, S * t:S * (t + 1)], MULT)

        def put_h1(b, t):
            nc.vector.tensor_tensor(pages[PACK * b + t][:].indirect(idx3[:]), hh[t][:, S:2 * S], wgd[0][:, S * t:S * (t + 1)], MULT)

        make_identity(nc, ident[:])
        for plane in (tab2s, tabs, w2s, w4s_raw):
            nc.vector.memset(plane[:].bitcast(I32), 0)

        nc.sync.dma_start(idx2[:], offs2)
        nc.sync.dma_start(out=cal_t[:], in_=cal.rearrange("(b p t) -> p b t", b=2, t=PACK))
        nc.sync.dma_start(idx4[:], offs4)
        nc.sync.dma_start(out=wg_raw[:], in_=wg2)
        load_rows(raw[0][:], w3[:, 0:KP])
        for r in range(4):
            nc.sync.dma_start(out=tab2s[r:P:32, :].bitcast(I32), in_=tab2_scales[0, r:16:4, :].bitcast(I32))
        nc.scalar.activation(warm[:], ident[:, 0:1], ACT.Silu)
        load_words(tab2w, tab2_words[0])
        load_page(0)
        load_page(1)
        deal_wg(1, banks[7], [raw[2][:, S * t:S * (t + 1)] for t in range(PACK)], banks[0:4])
        nc.sync.dma_start(out=wg_raw[:], in_=wg1)
        nc.sync.dma_start(idx[:], offs)
        load_words(tabw[0], tab_words[0])
        for r in range(4):
            nc.sync.dma_start(out=tabs[r:P:32, :, :].bitcast(I32),
                              in_=tab_scales[:, r:16:4, :].rearrange("a q t -> q a t").bitcast(I32))
        load_page(2)

        quant_w3("v", raw[0])
        nc.vector.tensor_copy(v2s[:], tab2s[:].indirect(idx2[:]))
        nc.vector.tensor_copy(v2w[:], tab2w[:].bitcast(U32).indirect(idx2[:]))
        for t in range(PACK):
            make_h2(0, t)
        deal_wg(0, banks[6], [stg[1 + t // 2][:].bitcast(F32)[:, S * (t % 2):S * (t % 2 + 1)] for t in range(PACK)], banks[0:4])
        for t in range(2):
            put_h2(0, t)
        nc.vector.tensor_copy(vw[0][:], tabw[0][:].bitcast(U32).indirect(idx[:]))
        for a in range(2):
            nc.vector.tensor_copy(vs[a][:], tabs[:, a, :].indirect(idx[:]))
        put_h2(0, 2)

        load_rows(raw[0][:], w3[:, KP:2 * KP])
        load_page(3)
        load_words(tabw[1], tab_words[1])
        load_page(4)
        load_w2_words(0)
        for r in range(4):
            nc.sync.dma_start(out=w2s[r:P:32, :, :].bitcast(I32),
                              in_=w2_scales[:, r:16:4, :].rearrange("a q t -> q a t").bitcast(I32))
        load_page(5)
        load_rows(raw[1][:], w1[0:KP, 0:KP])
        load_rows(w1_second, w1[KP:2 * KP, 0:KP])
        load_page(6)
        nc.sync.dma_start(idx3[:], offs3)
        load_page(7)
        nc.sync.dma_start(idx5[:], offs5)
        nc.sync.dma_start(out=gain_t[:], in_=gain.rearrange("(b p t) -> p b t", b=2, t=PACK))
        load_w2_words(1)

        quant_w3("s", raw[0])
        put_h2(0, 3)
        nc.vector.tensor_copy(vw[1][:], tabw[1][:].bitcast(U32).indirect(idx[:]))
        for t in range(PACK):
            make_h2(1, t)
        make_lin(0)
        for t in range(2):
            put_h2(1, t)
        quant_w1("v", 0, raw[1][:])
        quant_w1("s", 1, w1_second)
        for t in range(2, 4):
            put_h2(1, t)
        make_silu(0)
        for t in range(2):
            fetch_h1(t)

        w1_last = h_all[:, 2 * 2 * S:4 * 2 * S]
        load_rows(raw[1][:], w1[0:KP, KP:2 * KP])
        load_rows(w1_last, w1[KP:2 * KP, KP:2 * KP])
        nc.sync.dma_start(out=w4w_raw[:].rearrange("p (a c) -> p a c", a=2),
                          in_=w4_words.rearrange("a p c t -> p a (c t)").bitcast(I32))
        for q in range(4):
            nc.sync.dma_start(out=w4s_raw[32 * q:32 * q + 8, :].bitcast(I32), in_=w4_scales[:, 4 * q:4 * q + 4, :].bitcast(I32))
        load_rows(raw[0][:], w5)

        def read_page(t):
            nc.vector.tensor_copy(hh[t], pages[t][:].indirect(idx5[:]))
            if t < 2:
                bent = h_all[:, 4 * S:12 * S].rearrange("p (u x) -> p u x", u=2)[:, :, 2 * S * t:2 * S * t + S]
            else:
                bent = raw[1].rearrange("p (u x) -> p u x", u=2)[:, :, S * (3 - t):S * (4 - t)]
            nc.scalar.activation(bent, hh[t].rearrange("p (u x) -> p u x", u=2), ACT.Tanh)
            nc.scalar.activation(xb[:, t, :].rearrange("p (u x) -> p u x", u=2), bent, ACT.Copy, scale=gain_t[:, 0, t:t + 1])

        quant_w1("s", 0, raw[1][:])
        quant_w1("s", 1, w1_last)
        for t in range(2, 4):
            fetch_h1(t)
        make_lin(1)
        for t in range(2):
            put_h1(0, t)
            read_page(t)
        tide_raw = [alloc_big("tide_raw%d" % h) for h in range(2)]
        for h in range(2):
            load_rows(tide_raw[h][:], tide[:, KP * h:KP * (h + 1)])

        def quant_tide(h):
            cols = slice(KP * h, KP * (h + 1))
            weave("s", stg[1 + h][:], rows_view(tide_raw[h][:]))
            quant(tdc[:, cols], tds[:, cols], stg[1 + h][:])

        dst, src = cast_dealt_views(stg[0], raw[0])
        nc.scalar.activation(dst, src, ACT.Copy, scale=-1.0)
        quant(w5c[:], w5s[:], stg[0][:])
        quant_tide(0)
        make_silu(1)
        for t in range(2):
            fetch_h1(t)
        quant_tide(1)
        put_h1(0, 2)
        read_page(2)
        put_h1(0, 3)
        read_page(3)
        for h in range(2):
            cols = slice(KP * h, KP * (h + 1))
            weave("s", stg[3 + h][:], xb[:, :, cols])
            quant(xc[0][:, cols], xs[0][:, cols], stg[3 + h][:])
        fetch_h1(2)
        w4w = [alloc("w4w%d" % a, [P, KP], I32, tag="w1c%d" % a) for a in range(2)]
        w4s = alloc("w4s", [P, KP], U8, tag="w1s0")
        for a in range(2):
            nc.vector.tensor_copy(w4w[a][:].rearrange("p (t q) -> p q t", t=PACK),
                                  w4w_raw[:, KP * a:KP * (a + 1)].rearrange("p (q t) -> p q t", t=PACK))
        nc.vector.tensor_copy(w4s[:].rearrange("p (t q) -> p q t", t=PACK), w4s_raw[:].rearrange("p (q t) -> p q t", t=PACK))
        for t in range(PACK):
            put_h1(1, t)
            if t < PACK - 1:
                nc.vector.tensor_copy(hh[t], pages[PACK + t][:].indirect(idx5[:]))
                nc.scalar.activation(hh[t], hh[t], ACT.Tanh)
                nc.scalar.activation(xb[:, t, :], hh[t], ACT.Copy, scale=gain_t[:, 1, t:t + 1])
            if t == 1:
                fetch_h1(3)
                for h in range(2):
                    weave_pair("s", stg[1 + h][:], xb[:, :, KP * h:KP * (h + 1)], 0)

        def e_pass(jq, t, a, stop):
            cols = slice(QW * jq, QW * (jq + 1))
            out = banks[2 * jq + t // 2][:, QW * (t % 2):QW * (t % 2 + 1)]
            mm(out, w4w[a][:, P * t:P * (t + 1)].bitcast(FP8X4), w4s[4 * a:P, P * t:P * (t + 1)],
               xc[a][:, cols].bitcast(FP8X4), xs[a][:, cols], False, stop)

        for jq in range(NQ):
            cols = slice(QW * jq, QW * (jq + 1))
            for t in range(PACK):
                out = banks[2 * jq + t // 2][:, QW * (t % 2):QW * (t % 2 + 1)]
                mm(out, w5c[:, P * t:P * (t + 1)].bitcast(FP8X4), w5s[:, P * t:P * (t + 1)],
                   tdc[:, cols].bitcast(FP8X4), tds[:, cols], t % 2 == 0, False)
        for jq in range(NQ):
            for t in range(PACK):
                e_pass(jq, t, 0, False)

        y_rows = out_0.rearrange("(p t) j -> p t j", t=PACK)
        y_words = out_1[0].rearrange("p m t -> p (m t)").bitcast(I32)

        def make_x(jq):
            cols = slice(QW * jq, QW * (jq + 1))
            last = PACK - 1
            got = hh[last][:, cols]
            nc.vector.tensor_copy(got, pages[PACK + last][:].indirect(idx5[:, 16 * jq:16 * (jq + 1)]))
            bent = hh[last - 1][:, cols]
            nc.scalar.activation(bent, got, ACT.Tanh)
            nc.scalar.activation(xb[:, last, cols], bent, ACT.Copy, scale=gain_t[:, 1, last:last + 1])

        def make_y(jq):
            cols = slice(QW * jq, QW * (jq + 1))
            woven = stg[1 + jq // 2][:, J * (jq % 2):J * (jq % 2 + 1)]
            weave_pair("v", woven, xb[:, :, cols], 1)
            quant(xc[1][:, cols], xs[1][:, cols], woven)
            y = raw[jq // 2][:, J * (jq % 2):J * (jq % 2 + 1)]
            for t in range(PACK):
                e_pass(jq, t, 1, t % 2 == 1)
            for th in range(2):
                nc.scalar.activation(y[:, S * th:S * (th + 1)], banks[2 * jq + th][:], ACT.Abs)
                nc.sync.dma_start(out=y_rows[:, 2 * th:2 * th + 2, cols],
                                  in_=y[:, S * th:S * (th + 1)].rearrange("p (t j) -> p t j", t=2))

        def make_planes(jq):
            cols = slice(QW * jq, QW * (jq + 1))
            woven = stg[3 + jq // 2][:, J * (jq % 2):J * (jq % 2 + 1)]
            y = raw[jq // 2][:, J * (jq % 2):J * (jq % 2 + 1)]
            weave("v", woven, y.rearrange("p (t j) -> p t j", t=PACK))
            quant(yc[:, cols], ys[:, cols], woven)
            nc.sync.dma_start(out=y_words[:, cols], in_=yc[:, cols].bitcast(I32))

        for jq in range(NQ):
            make_x(jq)
        for step in range(NQ + 1):
            if step < NQ:
                make_y(step)
            if step >= 1:
                make_planes(step - 1)
        for r in range(4):
            queue = nc.sync if r % 2 == 0 else nc.scalar
            queue.dma_start(out=out_2[0, r:16:4, :].bitcast(I32), in_=ys[r:P:32, :].bitcast(I32))
